import numpy as np
import ml_dtypes


def mxq(x, axis, fmt="e4m3"):
    dtype, down = {"e4m3": (ml_dtypes.float8_e4m3fn, 7), "e5m2": (ml_dtypes.float8_e5m2, 14)}[fmt]
    v = np.moveaxis(np.asarray(x, np.float32).astype(ml_dtypes.bfloat16).astype(np.float64), axis, -1)
    blocks = v.reshape(v.shape[:-1] + (-1, 32))
    amax = np.abs(blocks).max(-1, keepdims=True)
    byte = np.maximum(np.where(amax > 0, np.frexp(amax)[1] - 1 + 127, 0) - down, 1)
    scale = np.exp2(byte - 127.0)
    codes = (blocks / scale).astype(np.float32).astype(dtype).astype(np.float64)
    return np.moveaxis((codes * scale).reshape(v.shape), -1, axis)


WIDE = False


def mx_kscale(k):
    if not WIDE:
        return np.ones(k)
    levels = np.array([10, -10, 5, -5, 0])
    if k % 512:
        return np.exp2(np.random.permutation(np.resize(levels, k // 32))).repeat(32)
    a = np.empty((k // 512, 16))
    for p in range(k // 512):
        a[p, :8] = np.random.permutation(np.resize(levels, 8))
        for g in range(8):
            far = levels[np.abs(levels - a[p, g]) >= 10]
            a[p, g + 8] = far[np.random.randint(len(far))]
    return np.exp2(a.ravel()).repeat(32)


BF16 = ml_dtypes.bfloat16


def bf(x):
    return np.asarray(x, np.float32).astype(BF16)


def f64(x):
    return np.asarray(x).astype(np.float64)


E2M1 = np.array([0.0, 0.5, 1.0, 1.5, 2.0, 3.0, 4.0, 6.0, -0.0, -0.5, -1.0, -1.5, -2.0, -3.0, -4.0, -6.0])


def pack_weight(w, fmt):
    k, n = w.shape
    w = f64(bf(w)).reshape(k // 32, 32, n)
    amax = np.abs(w).max(1)
    if fmt == "e4m3":
        byte = np.frexp(amax)[1] - 1 + 127 - 7
    else:
        mant, ex = np.frexp(amax / 6.0)
        byte = np.where(mant > 0.5, ex, ex - 1) + 127
    byte = np.clip(np.where(amax > 0, byte, 1), 1, 254)
    scaled = (w * np.exp2(127.0 - byte)[:, None, :]).reshape(k, n).astype(np.float32)
    by_word = np.ascontiguousarray(scaled.reshape(k // 512, 128, 4, n).transpose(0, 1, 3, 2))
    if fmt == "e4m3":
        words = by_word.astype(ml_dtypes.float8_e4m3fn).view(np.uint8)
    else:
        c = by_word.astype(ml_dtypes.float4_e2m1fn).view(np.uint8) & 0xF
        words = c[..., 0::2] | (c[..., 1::2] << 4)
    return np.ascontiguousarray(words), np.ascontiguousarray(byte.astype(np.uint8).reshape(k // 512, 16, n))


def unpack_weight(words, scales, fmt):
    g, p, n, _ = words.shape
    if fmt == "e4m3":
        vals = np.ascontiguousarray(words).view(ml_dtypes.float8_e4m3fn).astype(np.float64)
    else:
        nib = np.empty((g, p, n, 4), np.uint8)
        nib[..., 0::2] = words & 0xF
        nib[..., 1::2] = words >> 4
        vals = E2M1[nib]
    vals = vals * np.repeat(np.exp2(scales.astype(np.float64) - 127.0), 8, axis=1)[..., None]
    return vals.transpose(0, 1, 3, 2).reshape(g * 512, n)
def pack4(w):
    words, scales = pack_weight(w, "e2m1")
    return words.reshape(words.shape[0], 128, -1), scales


def unpack4(words, scales):
    return unpack_weight(words.reshape(words.shape[0], 128, -1, 2), scales, "e2m1")


E4M3FN = np.array([(-1.0 if i & 128 else 1.0) * ((1.0 + (i & 7) / 8.0) * 2.0 ** (((i >> 3) & 15) - 7) if i & 120 else (i & 7) * 2.0 ** -9) for i in range(256)])


def e4m3fn_bytes(y):
    return np.clip(np.asarray(y, np.float64), -448.0, 448.0).astype(np.float32).astype(ml_dtypes.float8_e4m3fn).view(np.uint8)


def e4m3fn_values(b):
    return E4M3FN[b]


A, K, H, R, B = 2048, 1536, 1024, 512, 128


def setup_inputs():
    s, t = mx_kscale(K), mx_kscale(H)
    x = np.random.standard_normal((A, K)) * s
    x_scale = (np.abs(x).reshape(A, K // B, B).max(axis=2) / 448).astype(np.float32)
    x_bytes = e4m3fn_bytes(x / np.repeat(f64(x_scale), B, axis=1))
    w = np.random.standard_normal((H, K)) / np.sqrt(K) / s
    v_words, v_scales = pack4(np.random.standard_normal((H, R)) / np.sqrt(H) / t[:, None])
    return {"x_bytes": x_bytes, "x_scale": x_scale,
            "w": bf(w),
            "bias": bf(0.3 * np.random.standard_normal(H)),
            "gain": bf((1 + 0.1 * np.random.standard_normal(H)) * t),
            "v_words": v_words, "v_scales": v_scales,
            "offset": bf(0.3 * np.random.standard_normal(R))}


def reference(x_bytes, x_scale, w, bias, gain, v_words, v_scales, offset):
    x = e4m3fn_values(x_bytes) * np.repeat(f64(x_scale), B, axis=1)
    z = mxq(x, 1, "e4m3") @ mxq(f64(w), 1, "e4m3").T
    h = np.tanh(z + f64(bias)) * f64(gain)
    v = unpack4(v_words, v_scales)
    return (mxq(h, 1, "e4m3") @ v) + f64(offset)

@@ -1,0 +1,300 @@
+from contextlib import ExitStack
+
+import concourse.mybir as mybir
+from concourse.masks import make_identity
+
+A, K, H, R, B = 2048, 1536, 1024, 512, 128
+FLOPS = 2 * A * K * H + 2 * A * H * R
+
+F32 = mybir.dt.float32
+BF16 = mybir.dt.bfloat16
+I32 = mybir.dt.int32
+U32 = mybir.dt.uint32
+U8 = mybir.dt.uint8
+FP8 = mybir.dt.float8_e4m3fn
+FP8X4 = mybir.dt.float8_e4m3fn_x4
+FP4X4 = mybir.dt.float4_e2m1fn_x4
+ACT = mybir.ActivationFunctionType
+ALU = mybir.AluOpType
+
+P = 128
+PASSES = K // 512
+GROUPS = H // 512
+ROWS = A // P
+UNITS = ROWS // 2
+BLOCKS = K // B
+
+
+def tile_atomic_energy_ensemble_d4_kernel(
+    tc, x_bytes, x_scale, w, bias, gain, v_words, v_scales, offset, out
+):
+    nc = tc.nc
+    with ExitStack() as ctx:
+        keep = ctx.enter_context(tc.tile_pool(name="keep", bufs=1))
+        work = ctx.enter_context(tc.tile_pool(name="work", bufs=3))
+        turn_psum = ctx.enter_context(tc.psum_pool(name="turn_psum", bufs=3))
+        z_psum = ctx.enter_context(tc.psum_pool(name="z_psum", bufs=3))
+        o_psum = ctx.enter_context(tc.psum_pool(name="o_psum", bufs=2))
+
+        ident = keep.tile([P, P], F32)
+        scale = keep.tile([P, ROWS, BLOCKS], F32)
+        x_raw = keep.tile([P, ROWS, K], U8)
+        w_raw = keep.tile([P, 4, 2, K], BF16, align_bytes=64)
+        w_codes = keep.tile([P, 4, PASSES, 2 * P], U32, align_bytes=64)
+        w_planes = keep.tile([P, 4, PASSES, 2 * P], U8, align_bytes=64)
+        bias_sb = keep.tile([P, GROUPS, 4], BF16)
+        gain_sb = keep.tile([P, GROUPS, 4], BF16)
+        v_sb = keep.tile([P, GROUPS, 2 * R], U8, align_bytes=64)
+        v_planes = keep.tile([P, GROUPS, R], U8, align_bytes=64)
+        offset_sb = keep.tile([P, R], BF16)
+        warm = keep.tile([P, 1], F32)
+
+        x_view = x_bytes.rearrange("(p n) k -> p n k", n=ROWS)
+        w_view = w.rearrange("(g m t) k -> g t m k", m=P, t=4)
+        out_view = out.rearrange("(p n) r -> n p r", n=ROWS)
+
+        def load_x(i):
+            nc.sync.dma_start(out=x_raw[:, 2 * i : 2 * i + 2, :], in_=x_view[:, 2 * i : 2 * i + 2, :])
+
+        def load_w(j, r):
+            g, h = divmod(j, 2)
+            nc.sync.dma_start(out=w_raw[:, j, r, :], in_=w_view[g, 2 * h + r])
+
+        def widen(i, r, b, engine):
+            n = 2 * i + r
+            src = x_raw[:, n, B * b : B * (b + 1)].bitcast(FP8)
+            s = scale[:, n, b : b + 1]
+            if engine == "v":
+                c, q = divmod(b, 4)
+                pairs = wide[i][:, r, 512 * c : 512 * (c + 1)].rearrange("p (u a e) -> p a u e", u=2, e=2)
+                nc.vector.tensor_scalar(
+                    out=pairs[:, 32 * q : 32 * (q + 1), :, :],
+                    in0=src.rearrange("p (a u e) -> p a u e", u=2, e=2),
+                    scalar1=s,
+                    scalar2=None,
+                    op0=ALU.mult,
+                )
+                sorted_words.add((i, r, c))
+            else:
+                nc.scalar.activation(out=wide[i][:, r, B * b : B * (b + 1)], in_=src, func=ACT.Copy, scale=s)
+
+        def new_wide(i):
+            x_wide = work.tile([P, 2, K], BF16, align_bytes=64)
+            wide[i] = x_wide
+
+        def turn(src, key, c, engine):
+            bank = turn_psum.tile([P, 2, 2, P], F32)
+            for r in range(2):
+                words = src[:, r, :].bitcast(F32)
+                for u in range(2):
+                    if key[0] == "x" and (key[1], r, c) in sorted_words:
+                        picked = words[:, 256 * c + P * u : 256 * c + P * (u + 1)]
+                    else:
+                        picked = words[:, 256 * c + u : 256 * (c + 1) : 2]
+                    nc.tensor.transpose(bank[:, r, u, :], picked, ident[:])
+            grouped = work.tile([P, 2, P, 4], BF16, align_bytes=64, bufs=9)
+            o = grouped[:].bitcast(F32)
+            i_ = bank[:].rearrange("p r u n -> p r n u")
+            if engine == "v":
+                nc.vector.tensor_copy(out=o, in_=i_)
+            else:
+                nc.scalar.copy(out=o, in_=i_)
+            groups[(key, c)] = grouped
+
+        def quantize(key, c, codes, planes):
+            nc.vector.quantize_mx(
+                out=codes.bitcast(FP8X4),
+                scales=planes,
+                in_=groups[(key, c)][:].rearrange("p r n t -> p (r n t)"),
+            )
+
+        def quantize_x(i, c):
+            if c == 0:
+                x_codes = work.tile([P, PASSES, 2 * P], U32, align_bytes=64)
+                x_planes = work.tile([P, PASSES, 2 * P], U8, align_bytes=64)
+                xq[i] = (x_codes, x_planes)
+            quantize(("x", i), c, xq[i][0][:, c, :], xq[i][1][:, c, :])
+
+        def quantize_w(j, c):
+            quantize(("w", j), c, w_codes[:, j, c, :], w_planes[:, j, c, :])
+
+        def product_1(i, j):
+            z = z_psum.tile([P, 2, 2 * P], F32)
+            for r in range(2):
+                for c in range(PASSES):
+                    nc.tensor.matmul_mx(
+                        out=z[:, r, :],
+                        lhsT=w_codes[:, j, c, r * P : (r + 1) * P].bitcast(FP8X4),
+                        lhsT_scale=w_planes[:, j, c, r * P : (r + 1) * P],
+                        rhs=xq[i][0][:, c, :].bitcast(FP8X4),
+                        rhs_scale=xq[i][1][:, c, :],
+                        start=(c == 0),
+                        stop=(c == PASSES - 1),
+                    )
+            zs[(i, j)] = z
+
+        def tanh(i, j):
+            g, h = divmod(j, 2)
+            if h == 0:
+                h_tanh = work.tile([P, 4, 2 * P], F32)
+                hidden[(i, g)] = h_tanh
+            for r in range(2):
+                t = 2 * h + r
+                nc.scalar.activation(
+                    out=hidden[(i, g)][:, t, :], in_=zs[(i, j)][:, r, :], func=ACT.Tanh, bias=bias_sb[:, g, t : t + 1]
+                )
+
+        def times_gain(i, g):
+            h_grouped = work.tile([P, 2 * P, 4], BF16, align_bytes=64)
+            nc.vector.tensor_tensor(
+                out=h_grouped[:].rearrange("p (c i) t -> p c t i", i=4),
+                in0=hidden[(i, g)][:].rearrange("p t (c i) -> p c t i", i=4),
+                in1=gain_sb[:, g, :].unsqueeze(1).unsqueeze(3).to_broadcast([P, 2 * P // 4, 4, 4]),
+                op=ALU.mult,
+            )
+            gained[(i, g)] = h_grouped
+
+        def quantize_h(i, g):
+            h_codes = work.tile([P, 2 * P], U32, align_bytes=64, bufs=6)
+            h_planes = work.tile([P, 2 * P], U8, align_bytes=64, bufs=6)
+            nc.vector.quantize_mx(
+                out=h_codes[:].bitcast(FP8X4),
+                scales=h_planes[:],
+                in_=gained[(i, g)][:].rearrange("p n t -> p (n t)"),
+            )
+            hq[(i, g)] = (h_codes, h_planes)
+
+        def product_2(i, r):
+            o = o_psum.tile([P, R], F32)
+            for g in range(GROUPS):
+                codes, planes = hq[(i, g)]
+                nc.tensor.matmul_mx(
+                    out=o[:],
+                    lhsT=codes[:, r * P : (r + 1) * P].bitcast(FP8X4),
+                    lhsT_scale=planes[:, r * P : (r + 1) * P],
+                    rhs=v_sb[:, g, :].bitcast(FP4X4),
+                    rhs_scale=v_planes[:, g, :],
+                    start=(g == 0),
+                    stop=(g == GROUPS - 1),
+                )
+            outs[(i, r)] = o
+
+        def finish(i, r):
+            energies = work.tile([P, R], F32, bufs=4)
+            nc.vector.tensor_tensor(out=energies[:], in0=outs[(i, r)][:], in1=offset_sb[:], op=ALU.add)
+            nc.sync.dma_start(out=out_view[2 * i + r], in_=energies[:])
+
+        sorted_words = set()
+        wide, groups, xq, zs, hidden, gained, hq, outs = {}, {}, {}, {}, {}, {}, {}, {}
+
+        with tc.manual_schedule():
+            nc.vector.memset(warm[:], 0.0)
+            nc.scalar.activation(out=warm[:], in_=warm[:], func=ACT.Tanh)
+            make_identity(nc, ident[:])
+            nc.gpsimd.memset(v_planes[:].rearrange("p g n -> p (g n)").bitcast(I32), 0)
+
+            nc.sync.dma_start(out=scale[:], in_=x_scale.rearrange("(p n) j -> p n j", n=ROWS))
+            load_x(0)
+            load_w(0, 0)
+            load_w(0, 1)
+            load_w(1, 0)
+            load_w(1, 1)
+            load_x(1)
+            nc.sync.dma_start(out=bias_sb[:], in_=bias.rearrange("(g p t) -> p g t", p=P, t=4))
+            load_w(2, 0)
+            load_w(2, 1)
+            nc.sync.dma_start(out=gain_sb[:], in_=gain.rearrange("(g p t) -> p g t", p=P, t=4))
+            load_w(3, 0)
+            load_w(3, 1)
+            load_x(2)
+            for q in range(4):
+                nc.sync.dma_start(
+                    out=v_planes[32 * q : 32 * q + 4, :, :].bitcast(I32),
+                    in_=v_scales[:, 4 * q : 4 * q + 4, :].rearrange("g q n -> q g n").bitcast(I32),
+                )
+            nc.sync.dma_start(out=v_sb[:].bitcast(I32), in_=v_words.rearrange("g p n -> p g n").bitcast(I32))
+            load_x(3)
+            nc.sync.dma_start(out=offset_sb[:], in_=offset.partition_broadcast(P))
+            for i in range(4, UNITS):
+                load_x(i)
+
+            def turn_all(src, key, engines):
+                for c in range(PASSES):
+                    turn(src, key, c, engines[c])
+
+            new_wide(0)
+            for b in range(BLOCKS):
+                widen(0, 0, b, "v")
+                widen(0, 1, b, "v" if b < 4 else "s")
+            turn_all(w_raw[:, 0, :, :], ("w", 0), "vsv")
+            turn_all(wide[0], ("x", 0), "svs")
+            for c in range(PASSES):
+                quantize_w(0, c)
+            turn_all(w_raw[:, 1, :, :], ("w", 1), "svs")
+            for c in range(PASSES):
+                quantize_x(0, c)
+            product_1(0, 0)
+            new_wide(1)
+            for b in range(BLOCKS):
+                widen(1, 0, b, "v")
+                if b == 5:
+                    for c in range(PASSES):
+                        quantize_w(1, c)
+            turn_all(w_raw[:, 2, :, :], ("w", 2), "svs")
+            tanh(0, 0)
+            for b in range(BLOCKS):
+                widen(1, 1, b, "v" if b < 8 else "s")
+            product_1(0, 1)
+            for c in range(PASSES):
+                quantize_w(2, c)
+            turn_all(w_raw[:, 3, :, :], ("w", 3), "svs")
+            tanh(0, 1)
+            product_1(0, 2)
+            for c in range(PASSES):
+                quantize_w(3, c)
+            turn_all(wide[1], ("x", 1), "svs")
+            tanh(0, 2)
+            times_gain(0, 0)
+            product_1(0, 3)
+
+            for i in range(UNITS):
+                ahead = i + 2
+                more = ahead < UNITS
+                if i + 1 < UNITS:
+                    for c in range(PASSES):
+                        quantize_x(i + 1, c)
+                if more:
+                    new_wide(ahead)
+                if i > 0:
+                    for j in range(4):
+                        product_1(i, j)
+                        tanh(i, j)
+                        if more:
+                            for b in range(3 * j, 3 * j + 3):
+                                widen(ahead, 0, b, "v")
+                                widen(ahead, 1, b, "s")
+                        if j == 1:
+                            times_gain(i, 0)
+                        if j == 2:
+                            quantize_h(i, 0)
+                    for r in range(2):
+                        product_2(i - 1, r)
+                    finish(i - 1, 0)
+                    times_gain(i, 1)
+                    finish(i - 1, 1)
+                    quantize_h(i, 1)
+                else:
+                    tanh(0, 3)
+                    for b in range(BLOCKS):
+                        widen(ahead, 0, b, "v")
+                        widen(ahead, 1, b, "s")
+                        if b == 2:
+                            quantize_h(0, 0)
+                        if b == 6:
+                            times_gain(0, 1)
+                    quantize_h(0, 1)
+                if more:
+                    turn_all(wide[ahead], ("x", ahead), "sss")
+            for r in range(2):
+                product_2(UNITS - 1, r)
+                finish(UNITS - 1, r)

@@ -24,6 +24,214 @@ ROWS = A // P
 UNITS = ROWS // 2
 BLOCKS = K // B
 
+PLAN = {
+    "v_rows": [[(0, 0), (0, 1), (0, 2), (1, 0), (1, 1), (1, 2)], [(0, 0), (0, 1), (0, 2)], [(0, 0), (0, 1), (0, 2)], [(0, 0), (0, 1), (0, 2)], [(0, 0), (0, 1), (0, 2), (1, 0), (1, 1)], [(0, 0), (0, 1), (0, 2), (1, 0)], [(0, 0), (0, 1)], [(0, 0), (0, 1), (0, 2), (1, 0)]],
+    "steps": [
+        ('D', 8),
+        ('V', 24),
+        ('S', 0),
+        ('TW', 0, 'svs'),
+        ('D', 1),
+        ('TX', 0, 'vss'),
+        ('QW', 0),
+        ('V', 1),
+        ('D', 1),
+        ('TW', 1, 'sss'),
+        ('QX', 0),
+        ('V', 10),
+        ('Z', 0, 0),
+        ('QW', 1),
+        ('S', 13),
+        ('TW', 2, 'vvs'),
+        ('TH', 0, 0),
+        ('V', 8),
+        ('S', 6),
+        ('Z', 0, 1),
+        ('QW', 2),
+        ('V', 10),
+        ('S', 4),
+        ('TW', 3, 'vsv'),
+        ('TH', 0, 1),
+        ('V', 2),
+        ('Z', 0, 2),
+        ('QW', 3),
+        ('S', 2),
+        ('TX', 1, 'svs'),
+        ('TH', 0, 2),
+        ('G', 0, 0),
+        ('V', 1),
+        ('Z', 0, 3),
+        ('QX', 1),
+        ('V', 2),
+        ('H', 0, 0),
+        ('TH', 0, 3),
+        ('TX', 2, 'sss'),
+        ('Q1', 2, 0),
+        ('Z', 1, 0),
+        ('TH', 1, 0),
+        ('G', 0, 1),
+        ('Q1', 2, 1),
+        ('Q1', 2, 2),
+        ('Z', 1, 1),
+        ('TH', 1, 1),
+        ('S', 2),
+        ('H', 0, 1),
+        ('G', 1, 0),
+        ('Z', 1, 2),
+        ('TH', 1, 2),
+        ('V', 15),
+        ('S', 2),
+        ('H', 1, 0),
+        ('Z', 1, 3),
+        ('TH', 1, 3),
+        ('S', 9),
+        ('O', 0, 0),
+        ('O', 0, 1),
+        ('A', 0, 0),
+        ('G', 1, 1),
+        ('A', 0, 1),
+        ('H', 1, 1),
+        ('TX', 3, 'sss'),
+        ('Q1', 3, 0),
+        ('Z', 2, 0),
+        ('TH', 2, 0),
+        ('Q1', 3, 1),
+        ('Q1', 3, 2),
+        ('Z', 2, 1),
+        ('TH', 2, 1),
+        ('S', 2),
+        ('G', 2, 0),
+        ('Z', 2, 2),
+        ('TH', 2, 2),
+        ('V', 15),
+        ('S', 2),
+        ('H', 2, 0),
+        ('Z', 2, 3),
+        ('TH', 2, 3),
+        ('S', 9),
+        ('O', 1, 0),
+        ('O', 1, 1),
+        ('A', 1, 0),
+        ('G', 2, 1),
+        ('A', 1, 1),
+        ('H', 2, 1),
+        ('TX', 4, 'sss'),
+        ('Q1', 4, 0),
+        ('Z', 3, 0),
+        ('TH', 3, 0),
+        ('Q1', 4, 1),
+        ('Q1', 4, 2),
+        ('Z', 3, 1),
+        ('TH', 3, 1),
+        ('S', 2),
+        ('G', 3, 0),
+        ('Z', 3, 2),
+        ('TH', 3, 2),
+        ('V', 15),
+        ('S', 2),
+        ('H', 3, 0),
+        ('Z', 3, 3),
+        ('TH', 3, 3),
+        ('S', 9),
+        ('O', 2, 0),
+        ('O', 2, 1),
+        ('A', 2, 0),
+        ('G', 3, 1),
+        ('A', 2, 1),
+        ('H', 3, 1),
+        ('TX', 5, 'sss'),
+        ('Q1', 5, 0),
+        ('Z', 4, 0),
+        ('TH', 4, 0),
+        ('Q1', 5, 1),
+        ('Q1', 5, 2),
+        ('Z', 4, 1),
+        ('TH', 4, 1),
+        ('S', 2),
+        ('G', 4, 0),
+        ('Z', 4, 2),
+        ('TH', 4, 2),
+        ('V', 15),
+        ('S', 2),
+        ('H', 4, 0),
+        ('Z', 4, 3),
+        ('TH', 4, 3),
+        ('S', 9),
+        ('O', 3, 0),
+        ('O', 3, 1),
+        ('A', 3, 0),
+        ('G', 4, 1),
+        ('A', 3, 1),
+        ('H', 4, 1),
+        ('TX', 6, 'sss'),
+        ('Q1', 6, 0),
+        ('Z', 5, 0),
+        ('TH', 5, 0),
+        ('Q1', 6, 1),
+        ('Q1', 6, 2),
+        ('Z', 5, 1),
+        ('TH', 5, 1),
+        ('S', 2),
+        ('G', 5, 0),
+        ('Z', 5, 2),
+        ('TH', 5, 2),
+        ('V', 15),
+        ('S', 2),
+        ('H', 5, 0),
+        ('Z', 5, 3),
+        ('TH', 5, 3),
+        ('S', 9),
+        ('O', 4, 0),
+        ('O', 4, 1),
+        ('A', 4, 0),
+        ('G', 5, 1),
+        ('A', 4, 1),
+        ('H', 5, 1),
+        ('TX', 7, 'sss'),
+        ('Q1', 7, 0),
+        ('Z', 6, 0),
+        ('TH', 6, 0),
+        ('Q1', 7, 1),
+        ('Q1', 7, 2),
+        ('Z', 6, 1),
+        ('TH', 6, 1),
+        ('G', 6, 0),
+        ('Z', 6, 2),
+        ('TH', 6, 2),
+        ('H', 6, 0),
+        ('Z', 6, 3),
+        ('TH', 6, 3),
+        ('O', 5, 0),
+        ('O', 5, 1),
+        ('A', 5, 0),
+        ('G', 6, 1),
+        ('A', 5, 1),
+        ('H', 6, 1),
+        ('Z', 7, 0),
+        ('TH', 7, 0),
+        ('Z', 7, 1),
+        ('TH', 7, 1),
+        ('G', 7, 0),
+        ('Z', 7, 2),
+        ('TH', 7, 2),
+        ('H', 7, 0),
+        ('O', 6, 0),
+        ('O', 6, 1),
+        ('A', 6, 0),
+        ('A', 6, 1),
+        ('Z', 7, 3),
+        ('TH', 7, 3),
+        ('GT', 7, 0),
+        ('GT', 7, 1),
+        ('HT', 7, 0),
+        ('HT', 7, 1),
+        ('O', 7, 0),
+        ('A', 7, 0),
+        ('O', 7, 1),
+        ('A', 7, 1),
+    ],
+}
+
 
 def tile_atomic_energy_ensemble_d4_kernel(
     tc, x_bytes, x_scale, w, bias, gain, v_words, v_scales, offset, out
@@ -48,6 +256,7 @@ def tile_atomic_energy_ensemble_d4_kernel(
         v_planes = keep.tile([P, GROUPS, R], U8, align_bytes=64)
         offset_sb = keep.tile([P, R], BF16)
         warm = keep.tile([P, 1], F32)
+        zeros = keep.tile([P, 5 * P], BF16)
 
         x_view = x_bytes.rearrange("(p n) k -> p n k", n=ROWS)
         w_view = w.rearrange("(g m t) k -> g t m k", m=P, t=4)
@@ -119,7 +328,7 @@ def tile_atomic_energy_ensemble_d4_kernel(
             quantize(("w", j), c, w_codes[:, j, c, :], w_planes[:, j, c, :])
 
         def product_1(i, j):
-            z = z_psum.tile([P, 2, 2 * P], F32)
+            z = z_psum.tile([P, 2, 2 * P], F32, tag="z")
             for r in range(2):
                 for c in range(PASSES):
                     nc.tensor.matmul_mx(
@@ -164,6 +373,32 @@ def tile_atomic_energy_ensemble_d4_kernel(
             )
             hq[(i, g)] = (h_codes, h_planes)
 
+        def times_gain_half(i, r):
+            g = 1
+            if r == 0:
+                h_grouped_t = work.tile([P, 2 * P, 4], BF16, align_bytes=64, bufs=1)
+                gained[(i, g)] = h_grouped_t
+            cols = slice(r * P, (r + 1) * P)
+            nc.vector.tensor_tensor(
+                out=gained[(i, g)][:, cols, :].rearrange("p (c i) t -> p c t i", i=4),
+                in0=hidden[(i, g)][:, :, cols].rearrange("p t (c i) -> p c t i", i=4),
+                in1=gain_sb[:, g, :].unsqueeze(1).unsqueeze(3).to_broadcast([P, P // 4, 4, 4]),
+                op=ALU.mult,
+            )
+
+        def quantize_h_half(i, r):
+            g = 1
+            if r == 0:
+                h_codes_t = work.tile([P, 2 * P], U32, align_bytes=64, bufs=1)
+                h_planes_t = work.tile([P, 2 * P], U8, align_bytes=64, bufs=1)
+                hq[(i, g)] = (h_codes_t, h_planes_t)
+            cols = slice(r * P, (r + 1) * P)
+            nc.vector.quantize_mx(
+                out=hq[(i, g)][0][:, cols].bitcast(FP8X4),
+                scales=hq[(i, g)][1][:, cols],
+                in_=gained[(i, g)][:, cols, :].rearrange("p n t -> p (n t)"),
+            )
+
         def product_2(i, r):
             o = o_psum.tile([P, R], F32)
             for g in range(GROUPS):
@@ -184,10 +419,80 @@ def tile_atomic_energy_ensemble_d4_kernel(
             nc.vector.tensor_tensor(out=energies[:], in0=outs[(i, r)][:], in1=offset_sb[:], op=ALU.add)
             nc.sync.dma_start(out=out_view[2 * i + r], in_=energies[:])
 
-        sorted_words = set()
         wide, groups, xq, zs, hidden, gained, hq, outs = {}, {}, {}, {}, {}, {}, {}, {}
+        sorted_words = set()
+        pending = {"v": [], "s": []}
+        for i in range(UNITS):
+            for c in range(PASSES):
+                for r in range(2):
+                    for q in range(4):
+                        pending["v" if (r, c) in PLAN["v_rows"][i] else "s"].append((i, r, 4 * c + q))
+
+        def fill(engine, count):
+            for n in range(min(count, len(pending[engine]))):
+                i, r, b = pending[engine].pop(0)
+                if i not in wide:
+                    new_wide(i)
+                widen(i, r, b, engine)
+
+        def flush(i, c):
+            for engine in ("v", "s"):
+                while pending[engine] and (pending[engine][0][0] < i or (pending[engine][0][0] == i and pending[engine][0][2] < 4 * (c + 1))):
+                    fill(engine, 1)
+
+        def turn_x(i, engines):
+            for c in range(PASSES):
+                flush(i, c)
+                turn(wide[i], ("x", i), c, engines[c])
+
+        def turn_w(j, engines):
+            for c in range(PASSES):
+                turn(w_raw[:, j, :, :], ("w", j), c, engines[c])
+
+        def heat():
+            bank = z_psum.tile([P, 512], F32, tag="z")
+            nc.tensor.matmul(bank[:], lhsT=zeros[:, :P], rhs=zeros[:, P:], start=True, stop=True)
+
+        def run(step):
+            name, args = step[0], step[1:]
+            if name == "V":
+                fill("v", args[0])
+            elif name == "S":
+                fill("s", args[0])
+            elif name == "TW":
+                turn_w(args[0], args[1])
+            elif name == "TX":
+                turn_x(args[0], args[1])
+            elif name == "QW":
+                for c in range(PASSES):
+                    quantize_w(args[0], c)
+            elif name == "QX":
+                for c in range(PASSES):
+                    quantize_x(args[0], c)
+            elif name == "Q1":
+                quantize_x(args[0], args[1])
+            elif name == "Z":
+                product_1(args[0], args[1])
+            elif name == "TH":
+                tanh(args[0], args[1])
+            elif name == "G":
+                times_gain(args[0], args[1])
+            elif name == "H":
+                quantize_h(args[0], args[1])
+            elif name == "O":
+                product_2(args[0], args[1])
+            elif name == "A":
+                finish(args[0], args[1])
+            elif name == "D":
+                for n in range(args[0]):
+                    heat()
+            elif name == "GT":
+                times_gain_half(args[0], args[1])
+            elif name == "HT":
+                quantize_h_half(args[0], args[1])
 
         with tc.manual_schedule():
+            nc.vector.memset(zeros[:], 0.0)
             nc.vector.memset(warm[:], 0.0)
             nc.scalar.activation(out=warm[:], in_=warm[:], func=ACT.Tanh)
             make_identity(nc, ident[:])
@@ -218,83 +523,5 @@ def tile_atomic_energy_ensemble_d4_kernel(
             for i in range(4, UNITS):
                 load_x(i)
 
-            def turn_all(src, key, engines):
-                for c in range(PASSES):
-                    turn(src, key, c, engines[c])
-
-            new_wide(0)
-            for b in range(BLOCKS):
-                widen(0, 0, b, "v")
-                widen(0, 1, b, "v" if b < 4 else "s")
-            turn_all(w_raw[:, 0, :, :], ("w", 0), "vsv")
-            turn_all(wide[0], ("x", 0), "svs")
-            for c in range(PASSES):
-                quantize_w(0, c)
-            turn_all(w_raw[:, 1, :, :], ("w", 1), "svs")
-            for c in range(PASSES):
-                quantize_x(0, c)
-            product_1(0, 0)
-            new_wide(1)
-            for b in range(BLOCKS):
-                widen(1, 0, b, "v")
-                if b == 5:
-                    for c in range(PASSES):
-                        quantize_w(1, c)
-            turn_all(w_raw[:, 2, :, :], ("w", 2), "svs")
-            tanh(0, 0)
-            for b in range(BLOCKS):
-                widen(1, 1, b, "v" if b < 8 else "s")
-            product_1(0, 1)
-            for c in range(PASSES):
-                quantize_w(2, c)
-            turn_all(w_raw[:, 3, :, :], ("w", 3), "svs")
-            tanh(0, 1)
-            product_1(0, 2)
-            for c in range(PASSES):
-                quantize_w(3, c)
-            turn_all(wide[1], ("x", 1), "svs")
-            tanh(0, 2)
-            times_gain(0, 0)
-            product_1(0, 3)
-
-            for i in range(UNITS):
-                ahead = i + 2
-                more = ahead < UNITS
-                if i + 1 < UNITS:
-                    for c in range(PASSES):
-                        quantize_x(i + 1, c)
-                if more:
-                    new_wide(ahead)
-                if i > 0:
-                    for j in range(4):
-                        product_1(i, j)
-                        tanh(i, j)
-                        if more:
-                            for b in range(3 * j, 3 * j + 3):
-                                widen(ahead, 0, b, "v")
-                                widen(ahead, 1, b, "s")
-                        if j == 1:
-                            times_gain(i, 0)
-                        if j == 2:
-                            quantize_h(i, 0)
-                    for r in range(2):
-                        product_2(i - 1, r)
-                    finish(i - 1, 0)
-                    times_gain(i, 1)
-                    finish(i - 1, 1)
-                    quantize_h(i, 1)
-                else:
-                    tanh(0, 3)
-                    for b in range(BLOCKS):
-                        widen(ahead, 0, b, "v")
-                        widen(ahead, 1, b, "s")
-                        if b == 2:
-                            quantize_h(0, 0)
-                        if b == 6:
-                            times_gain(0, 1)
-                    quantize_h(0, 1)
-                if more:
-                    turn_all(wide[ahead], ("x", ahead), "sss")
-            for r in range(2):
-                product_2(UNITS - 1, r)
-                finish(UNITS - 1, r)
+            for step in PLAN["steps"]:
+                run(step)

@@ -356,9 +356,9 @@ def tile_atomic_energy_ensemble_d4_kernel(
         def times_gain(i, g):
             h_grouped = work.tile([P, 2 * P, 4], BF16, align_bytes=64)
             nc.vector.tensor_tensor(
-                out=h_grouped[:].rearrange("p (c i) t -> p c t i", i=4),
-                in0=hidden[(i, g)][:].rearrange("p t (c i) -> p c t i", i=4),
-                in1=gain_sb[:, g, :].unsqueeze(1).unsqueeze(3).to_broadcast([P, 2 * P // 4, 4, 4]),
+                out=h_grouped[:].rearrange("p (c i) t -> p c t i", i=2),
+                in0=hidden[(i, g)][:].rearrange("p t (c i) -> p c t i", i=2),
+                in1=gain_sb[:, g, :].unsqueeze(1).unsqueeze(3).to_broadcast([P, P, 4, 2]),
                 op=ALU.mult,
             )
             gained[(i, g)] = h_grouped
@@ -380,9 +380,9 @@ def tile_atomic_energy_ensemble_d4_kernel(
                 gained[(i, g)] = h_grouped_t
             cols = slice(r * P, (r + 1) * P)
             nc.vector.tensor_tensor(
-                out=gained[(i, g)][:, cols, :].rearrange("p (c i) t -> p c t i", i=4),
-                in0=hidden[(i, g)][:, :, cols].rearrange("p t (c i) -> p c t i", i=4),
-                in1=gain_sb[:, g, :].unsqueeze(1).unsqueeze(3).to_broadcast([P, P // 4, 4, 4]),
+                out=gained[(i, g)][:, cols, :].rearrange("p (c i) t -> p c t i", i=2),
+                in0=hidden[(i, g)][:, :, cols].rearrange("p t (c i) -> p c t i", i=2),
+                in1=gain_sb[:, g, :].unsqueeze(1).unsqueeze(3).to_broadcast([P, P // 2, 4, 2]),
                 op=ALU.mult,
             )
 

@@ -25,66 +25,85 @@ UNITS = ROWS // 2
 BLOCKS = K // B
 
 PLAN = {
-    "v_rows": [[(0, 0), (0, 1), (0, 2), (1, 0), (1, 1), (1, 2)], [(0, 0), (0, 1), (0, 2)], [(0, 0), (0, 1), (0, 2)], [(0, 0), (0, 1), (0, 2)], [(0, 0), (0, 1), (0, 2), (1, 0), (1, 1)], [(0, 0), (0, 1), (0, 2), (1, 0)], [(0, 0), (0, 1)], [(0, 0), (0, 1), (0, 2), (1, 0)]],
+    "v_rows": [[(0, 0), (0, 1), (0, 2), (1, 0), (1, 1), (1, 2)], [(0, 0), (0, 1), (0, 2), (1, 0), (1, 1)], [(0, 0), (0, 1), (0, 2)], [(0, 0), (0, 1), (0, 2), (1, 0)], [(0, 0), (0, 1), (0, 2), (1, 0), (1, 1), (1, 2)], [(0, 0), (0, 1), (0, 2)], [(0, 0), (0, 1), (0, 2)], [(0, 0), (0, 1), (0, 2)]],
     "steps": [
-        ('D', 8),
+        ('D', 5),
         ('V', 24),
         ('S', 0),
-        ('TW', 0, 'svs'),
-        ('D', 1),
-        ('TX', 0, 'vss'),
+        ('T1', 'w', 0, 0, 's'),
+        ('T1', 'w', 0, 1, 's'),
+        ('T1', 'w', 0, 2, 's'),
+        ('V', 6),
+        ('D', 2),
+        ('T1', 'x', 0, 0, 's'),
+        ('T1', 'x', 0, 1, 'v'),
+        ('D', 2),
+        ('T1', 'x', 0, 2, 's'),
         ('QW', 0),
         ('V', 1),
-        ('D', 1),
-        ('TW', 1, 'sss'),
+        ('S', 4),
+        ('T1', 'w', 1, 0, 's'),
+        ('T1', 'w', 1, 1, 's'),
+        ('T1', 'w', 1, 2, 's'),
         ('QX', 0),
-        ('V', 10),
+        ('V', 19),
+        ('S', 3),
         ('Z', 0, 0),
         ('QW', 1),
-        ('S', 13),
-        ('TW', 2, 'vvs'),
+        ('V', 5),
+        ('T1', 'w', 2, 0, 'v'),
+        ('D', 2),
+        ('T1', 'w', 2, 1, 'v'),
+        ('T1', 'w', 2, 2, 'v'),
         ('TH', 0, 0),
-        ('V', 8),
-        ('S', 6),
+        ('V', 9),
+        ('S', 10),
         ('Z', 0, 1),
         ('QW', 2),
-        ('V', 10),
-        ('S', 4),
-        ('TW', 3, 'vsv'),
+        ('V', 5),
+        ('S', 3),
+        ('T1', 'w', 3, 0, 's'),
+        ('T1', 'w', 3, 1, 's'),
+        ('T1', 'w', 3, 2, 's'),
         ('TH', 0, 1),
-        ('V', 2),
+        ('S', 1),
         ('Z', 0, 2),
         ('QW', 3),
-        ('S', 2),
-        ('TX', 1, 'svs'),
+        ('T1', 'x', 1, 0, 'v'),
+        ('T1', 'x', 1, 1, 's'),
+        ('T1', 'x', 1, 2, 's'),
         ('TH', 0, 2),
         ('G', 0, 0),
-        ('V', 1),
         ('Z', 0, 3),
         ('QX', 1),
         ('V', 2),
         ('H', 0, 0),
         ('TH', 0, 3),
-        ('TX', 2, 'sss'),
+        ('V', 6),
+        ('T1', 'x', 2, 0, 's'),
+        ('T1', 'x', 2, 1, 's'),
+        ('T1', 'x', 2, 2, 's'),
         ('Q1', 2, 0),
         ('Z', 1, 0),
         ('TH', 1, 0),
         ('G', 0, 1),
         ('Q1', 2, 1),
         ('Q1', 2, 2),
+        ('V', 1),
         ('Z', 1, 1),
         ('TH', 1, 1),
-        ('S', 2),
+        ('V', 1),
+        ('S', 3),
         ('H', 0, 1),
         ('G', 1, 0),
         ('Z', 1, 2),
         ('TH', 1, 2),
-        ('V', 15),
-        ('S', 2),
+        ('V', 9),
+        ('S', 5),
         ('H', 1, 0),
         ('Z', 1, 3),
         ('TH', 1, 3),
-        ('S', 9),
+        ('V', 6),
         ('O', 0, 0),
         ('O', 0, 1),
         ('A', 0, 0),
@@ -97,18 +116,20 @@ PLAN = {
         ('TH', 2, 0),
         ('Q1', 3, 1),
         ('Q1', 3, 2),
+        ('V', 1),
         ('Z', 2, 1),
         ('TH', 2, 1),
-        ('S', 2),
+        ('V', 1),
+        ('S', 3),
         ('G', 2, 0),
         ('Z', 2, 2),
         ('TH', 2, 2),
-        ('V', 15),
-        ('S', 2),
+        ('V', 9),
+        ('S', 5),
         ('H', 2, 0),
         ('Z', 2, 3),
         ('TH', 2, 3),
-        ('S', 9),
+        ('V', 6),
         ('O', 1, 0),
         ('O', 1, 1),
         ('A', 1, 0),
@@ -121,18 +142,20 @@ PLAN = {
         ('TH', 3, 0),
         ('Q1', 4, 1),
         ('Q1', 4, 2),
+        ('V', 1),
         ('Z', 3, 1),
         ('TH', 3, 1),
-        ('S', 2),
+        ('V', 1),
+        ('S', 3),
         ('G', 3, 0),
         ('Z', 3, 2),
         ('TH', 3, 2),
-        ('V', 15),
-        ('S', 2),
+        ('V', 9),
+        ('S', 5),
         ('H', 3, 0),
         ('Z', 3, 3),
         ('TH', 3, 3),
-        ('S', 9),
+        ('V', 6),
         ('O', 2, 0),
         ('O', 2, 1),
         ('A', 2, 0),
@@ -145,18 +168,20 @@ PLAN = {
         ('TH', 4, 0),
         ('Q1', 5, 1),
         ('Q1', 5, 2),
+        ('V', 1),
         ('Z', 4, 1),
         ('TH', 4, 1),
-        ('S', 2),
+        ('V', 1),
+        ('S', 3),
         ('G', 4, 0),
         ('Z', 4, 2),
         ('TH', 4, 2),
-        ('V', 15),
-        ('S', 2),
+        ('V', 9),
+        ('S', 5),
         ('H', 4, 0),
         ('Z', 4, 3),
         ('TH', 4, 3),
-        ('S', 9),
+        ('V', 6),
         ('O', 3, 0),
         ('O', 3, 1),
         ('A', 3, 0),
@@ -169,18 +194,20 @@ PLAN = {
         ('TH', 5, 0),
         ('Q1', 6, 1),
         ('Q1', 6, 2),
+        ('V', 1),
         ('Z', 5, 1),
         ('TH', 5, 1),
-        ('S', 2),
+        ('V', 1),
+        ('S', 3),
         ('G', 5, 0),
         ('Z', 5, 2),
         ('TH', 5, 2),
-        ('V', 15),
-        ('S', 2),
+        ('V', 9),
+        ('S', 5),
         ('H', 5, 0),
         ('Z', 5, 3),
         ('TH', 5, 3),
-        ('S', 9),
+        ('V', 6),
         ('O', 4, 0),
         ('O', 4, 1),
         ('A', 4, 0),
@@ -215,12 +242,12 @@ PLAN = {
         ('Z', 7, 2),
         ('TH', 7, 2),
         ('H', 7, 0),
+        ('Z', 7, 3),
+        ('TH', 7, 3),
         ('O', 6, 0),
         ('O', 6, 1),
         ('A', 6, 0),
         ('A', 6, 1),
-        ('Z', 7, 3),
-        ('TH', 7, 3),
         ('GT', 7, 0),
         ('GT', 7, 1),
         ('HT', 7, 0),
@@ -318,7 +345,7 @@ def tile_atomic_energy_ensemble_d4_kernel(
             )
 
         def quantize_x(i, c):
-            if c == 0:
+            if i not in xq:
                 x_codes = work.tile([P, PASSES, 2 * P], U32, align_bytes=64)
                 x_planes = work.tile([P, PASSES, 2 * P], U8, align_bytes=64)
                 xq[i] = (x_codes, x_planes)
@@ -344,7 +371,7 @@ def tile_atomic_energy_ensemble_d4_kernel(
 
         def tanh(i, j):
             g, h = divmod(j, 2)
-            if h == 0:
+            if (i, g) not in hidden:
                 h_tanh = work.tile([P, 4, 2 * P], F32)
                 hidden[(i, g)] = h_tanh
             for r in range(2):
@@ -463,6 +490,15 @@ def tile_atomic_energy_ensemble_d4_kernel(
                 turn_w(args[0], args[1])
             elif name == "TX":
                 turn_x(args[0], args[1])
+            elif name == "T1":
+                kind, unit, c, engine = args
+                if kind == "w":
+                    turn(w_raw[:, unit, :, :], ("w", unit), c, engine)
+                else:
+                    flush(unit, c)
+                    turn(wide[unit], ("x", unit), c, engine)
+            elif name == "QW1":
+                quantize_w(args[0], args[1])
             elif name == "QW":
                 for c in range(PASSES):
                     quantize_w(args[0], c)
@@ -504,14 +540,14 @@ def tile_atomic_energy_ensemble_d4_kernel(
             load_w(0, 1)
             load_w(1, 0)
             load_w(1, 1)
-            load_x(1)
             nc.sync.dma_start(out=bias_sb[:], in_=bias.rearrange("(g p t) -> p g t", p=P, t=4))
+            load_x(1)
             load_w(2, 0)
             load_w(2, 1)
+            load_x(2)
             nc.sync.dma_start(out=gain_sb[:], in_=gain.rearrange("(g p t) -> p g t", p=P, t=4))
             load_w(3, 0)
             load_w(3, 1)
-            load_x(2)
             for q in range(4):
                 nc.sync.dma_start(
                     out=v_planes[32 * q : 32 * q + 4, :, :].bitcast(I32),

@@ -25,61 +25,59 @@ UNITS = ROWS // 2
 BLOCKS = K // B
 
 PLAN = {
-    "v_rows": [[(0, 0), (0, 1), (0, 2), (1, 0), (1, 1), (1, 2)], [(0, 0), (0, 1), (0, 2), (1, 0), (1, 1)], [(0, 0), (0, 1), (0, 2)], [(0, 0), (0, 1), (0, 2), (1, 0)], [(0, 0), (0, 1), (0, 2), (1, 0), (1, 1), (1, 2)], [(0, 0), (0, 1), (0, 2)], [(0, 0), (0, 1), (0, 2)], [(0, 0), (0, 1), (0, 2)]],
+    "v_rows": [[(0, 0), (0, 1), (0, 2), (1, 0), (1, 1), (1, 2)], [(0, 0), (0, 1), (0, 2), (1, 0)], [(0, 0), (0, 1), (0, 2), (1, 0), (1, 1)], [(0, 0), (0, 1), (0, 2), (1, 0)], [(0, 0), (0, 1), (0, 2), (1, 0)], [(0, 0), (0, 1), (0, 2)], [(0, 0)], [(0, 0), (0, 1), (0, 2), (1, 0), (1, 1)]],
+    "psum": (3, 3, 2),
     "steps": [
-        ('D', 5),
+        ('D', 4),
         ('V', 24),
         ('S', 0),
+        ('D', 2),
         ('T1', 'w', 0, 0, 's'),
         ('T1', 'w', 0, 1, 's'),
         ('T1', 'w', 0, 2, 's'),
-        ('V', 6),
-        ('D', 2),
+        ('V', 5),
         ('T1', 'x', 0, 0, 's'),
-        ('T1', 'x', 0, 1, 'v'),
-        ('D', 2),
+        ('T1', 'x', 0, 1, 's'),
         ('T1', 'x', 0, 2, 's'),
         ('QW', 0),
-        ('V', 1),
         ('S', 4),
+        ('D', 1),
         ('T1', 'w', 1, 0, 's'),
         ('T1', 'w', 1, 1, 's'),
         ('T1', 'w', 1, 2, 's'),
         ('QX', 0),
-        ('V', 19),
+        ('V', 15),
         ('S', 3),
         ('Z', 0, 0),
         ('QW', 1),
-        ('V', 5),
-        ('T1', 'w', 2, 0, 'v'),
-        ('D', 2),
-        ('T1', 'w', 2, 1, 'v'),
-        ('T1', 'w', 2, 2, 'v'),
+        ('V', 7),
+        ('S', 5),
+        ('T1', 'w', 2, 0, 's'),
+        ('T1', 'w', 2, 1, 's'),
+        ('T1', 'w', 2, 2, 's'),
         ('TH', 0, 0),
-        ('V', 9),
-        ('S', 10),
+        ('V', 7),
         ('Z', 0, 1),
         ('QW', 2),
-        ('V', 5),
-        ('S', 3),
         ('T1', 'w', 3, 0, 's'),
         ('T1', 'w', 3, 1, 's'),
         ('T1', 'w', 3, 2, 's'),
         ('TH', 0, 1),
+        ('V', 15),
         ('S', 1),
         ('Z', 0, 2),
         ('QW', 3),
-        ('T1', 'x', 1, 0, 'v'),
+        ('V', 3),
+        ('T1', 'x', 1, 0, 's'),
         ('T1', 'x', 1, 1, 's'),
         ('T1', 'x', 1, 2, 's'),
         ('TH', 0, 2),
         ('G', 0, 0),
         ('Z', 0, 3),
         ('QX', 1),
-        ('V', 2),
+        ('V', 8),
         ('H', 0, 0),
         ('TH', 0, 3),
-        ('V', 6),
         ('T1', 'x', 2, 0, 's'),
         ('T1', 'x', 2, 1, 's'),
         ('T1', 'x', 2, 2, 's'),
@@ -89,21 +87,19 @@ PLAN = {
         ('G', 0, 1),
         ('Q1', 2, 1),
         ('Q1', 2, 2),
-        ('V', 1),
         ('Z', 1, 1),
         ('TH', 1, 1),
-        ('V', 1),
-        ('S', 3),
+        ('S', 2),
         ('H', 0, 1),
         ('G', 1, 0),
         ('Z', 1, 2),
         ('TH', 1, 2),
-        ('V', 9),
-        ('S', 5),
+        ('V', 6),
+        ('S', 10),
         ('H', 1, 0),
         ('Z', 1, 3),
         ('TH', 1, 3),
-        ('V', 6),
+        ('V', 4),
         ('O', 0, 0),
         ('O', 0, 1),
         ('A', 0, 0),
@@ -116,20 +112,18 @@ PLAN = {
         ('TH', 2, 0),
         ('Q1', 3, 1),
         ('Q1', 3, 2),
-        ('V', 1),
         ('Z', 2, 1),
         ('TH', 2, 1),
-        ('V', 1),
-        ('S', 3),
+        ('S', 2),
         ('G', 2, 0),
         ('Z', 2, 2),
         ('TH', 2, 2),
-        ('V', 9),
-        ('S', 5),
+        ('V', 6),
+        ('S', 10),
         ('H', 2, 0),
         ('Z', 2, 3),
         ('TH', 2, 3),
-        ('V', 6),
+        ('V', 4),
         ('O', 1, 0),
         ('O', 1, 1),
         ('A', 1, 0),
@@ -142,20 +136,18 @@ PLAN = {
         ('TH', 3, 0),
         ('Q1', 4, 1),
         ('Q1', 4, 2),
-        ('V', 1),
         ('Z', 3, 1),
         ('TH', 3, 1),
-        ('V', 1),
-        ('S', 3),
+        ('S', 2),
         ('G', 3, 0),
         ('Z', 3, 2),
         ('TH', 3, 2),
-        ('V', 9),
-        ('S', 5),
+        ('V', 6),
+        ('S', 10),
         ('H', 3, 0),
         ('Z', 3, 3),
         ('TH', 3, 3),
-        ('V', 6),
+        ('V', 4),
         ('O', 2, 0),
         ('O', 2, 1),
         ('A', 2, 0),
@@ -168,20 +160,18 @@ PLAN = {
         ('TH', 4, 0),
         ('Q1', 5, 1),
         ('Q1', 5, 2),
-        ('V', 1),
         ('Z', 4, 1),
         ('TH', 4, 1),
-        ('V', 1),
-        ('S', 3),
+        ('S', 2),
         ('G', 4, 0),
         ('Z', 4, 2),
         ('TH', 4, 2),
-        ('V', 9),
-        ('S', 5),
+        ('V', 6),
+        ('S', 10),
         ('H', 4, 0),
         ('Z', 4, 3),
         ('TH', 4, 3),
-        ('V', 6),
+        ('V', 4),
         ('O', 3, 0),
         ('O', 3, 1),
         ('A', 3, 0),
@@ -194,20 +184,18 @@ PLAN = {
         ('TH', 5, 0),
         ('Q1', 6, 1),
         ('Q1', 6, 2),
-        ('V', 1),
         ('Z', 5, 1),
         ('TH', 5, 1),
-        ('V', 1),
-        ('S', 3),
+        ('S', 2),
         ('G', 5, 0),
         ('Z', 5, 2),
         ('TH', 5, 2),
-        ('V', 9),
-        ('S', 5),
+        ('V', 6),
+        ('S', 10),
         ('H', 5, 0),
         ('Z', 5, 3),
         ('TH', 5, 3),
-        ('V', 6),
+        ('V', 4),
         ('O', 4, 0),
         ('O', 4, 1),
         ('A', 4, 0),
@@ -238,23 +226,27 @@ PLAN = {
         ('TH', 7, 0),
         ('Z', 7, 1),
         ('TH', 7, 1),
+        ('ZH', 7, 0, 0),
+        ('THH', 7, 0, 0),
         ('G', 7, 0),
-        ('Z', 7, 2),
-        ('TH', 7, 2),
+        ('ZH', 7, 0, 1),
+        ('THH', 7, 0, 1),
         ('H', 7, 0),
-        ('Z', 7, 3),
-        ('TH', 7, 3),
+        ('ZH', 7, 1, 0),
+        ('THH', 7, 1, 0),
+        ('GT', 7, 0),
+        ('ZH', 7, 1, 1),
+        ('THH', 7, 1, 1),
         ('O', 6, 0),
         ('O', 6, 1),
-        ('A', 6, 0),
-        ('A', 6, 1),
-        ('GT', 7, 0),
-        ('GT', 7, 1),
         ('HT', 7, 0),
+        ('GT', 7, 1),
+        ('A', 6, 0),
         ('HT', 7, 1),
+        ('A', 6, 1),
         ('O', 7, 0),
-        ('A', 7, 0),
         ('O', 7, 1),
+        ('A', 7, 0),
         ('A', 7, 1),
     ],
 }
@@ -267,9 +259,9 @@ def tile_atomic_energy_ensemble_d4_kernel(
     with ExitStack() as ctx:
         keep = ctx.enter_context(tc.tile_pool(name="keep", bufs=1))
         work = ctx.enter_context(tc.tile_pool(name="work", bufs=3))
-        turn_psum = ctx.enter_context(tc.psum_pool(name="turn_psum", bufs=3))
-        z_psum = ctx.enter_context(tc.psum_pool(name="z_psum", bufs=3))
-        o_psum = ctx.enter_context(tc.psum_pool(name="o_psum", bufs=2))
+        turn_psum = ctx.enter_context(tc.psum_pool(name="turn_psum", bufs=PLAN["psum"][0]))
+        z_psum = ctx.enter_context(tc.psum_pool(name="z_psum", bufs=PLAN["psum"][1]))
+        o_psum = ctx.enter_context(tc.psum_pool(name="o_psum", bufs=PLAN["psum"][2]))
 
         ident = keep.tile([P, P], F32)
         scale = keep.tile([P, ROWS, BLOCKS], F32)
@@ -279,6 +271,7 @@ def tile_atomic_energy_ensemble_d4_kernel(
         w_planes = keep.tile([P, 4, PASSES, 2 * P], U8, align_bytes=64)
         bias_sb = keep.tile([P, GROUPS, 4], BF16)
         gain_sb = keep.tile([P, GROUPS, 4], BF16)
+        gain_f32 = keep.tile([P, GROUPS, 4], F32)
         v_sb = keep.tile([P, GROUPS, 2 * R], U8, align_bytes=64)
         v_planes = keep.tile([P, GROUPS, R], U8, align_bytes=64)
         offset_sb = keep.tile([P, R], BF16)
@@ -319,7 +312,7 @@ def tile_atomic_energy_ensemble_d4_kernel(
             wide[i] = x_wide
 
         def turn(src, key, c, engine):
-            bank = turn_psum.tile([P, 2, 2, P], F32)
+            bank = turn_psum.tile([P, 2, 2, P], F32, tag="turn")
             for r in range(2):
                 words = src[:, r, :].bitcast(F32)
                 for u in range(2):
@@ -380,8 +373,40 @@ def tile_atomic_energy_ensemble_d4_kernel(
                     out=hidden[(i, g)][:, t, :], in_=zs[(i, j)][:, r, :], func=ACT.Tanh, bias=bias_sb[:, g, t : t + 1]
                 )
 
+        def product_1_half(i, r, h):
+            if r == 0:
+                z_half = z_psum.tile([P, 2, P], F32, tag="z")
+            else:
+                z_half = turn_psum.tile([P, 2, P], F32, tag="turn")
+            cols = slice(r * P, (r + 1) * P)
+            for s in range(2):
+                for c in range(PASSES):
+                    nc.tensor.matmul_mx(
+                        out=z_half[:, s, :],
+                        lhsT=w_codes[:, 2 + h, c, s * P : (s + 1) * P].bitcast(FP8X4),
+                        lhsT_scale=w_planes[:, 2 + h, c, s * P : (s + 1) * P],
+                        rhs=xq[i][0][:, c, cols].bitcast(FP8X4),
+                        rhs_scale=xq[i][1][:, c, cols],
+                        start=(c == 0),
+                        stop=(c == PASSES - 1),
+                    )
+            zs[(i, r, h)] = z_half
+
+        def tanh_half(i, r, h):
+            if (i, 1, r) not in hidden:
+                h_tanh_half = work.tile([P, 4, P], F32, bufs=2)
+                hidden[(i, 1, r)] = h_tanh_half
+            for s in range(2):
+                t = 2 * h + s
+                nc.scalar.activation(
+                    out=hidden[(i, 1, r)][:, t, :],
+                    in_=zs[(i, r, h)][:, s, :],
+                    func=ACT.Tanh,
+                    bias=bias_sb[:, 1, t : t + 1],
+                )
+
         def times_gain(i, g):
-            h_grouped = work.tile([P, 2 * P, 4], BF16, align_bytes=64)
+            h_grouped = work.tile([P, 2 * P, 4], BF16, align_bytes=64, tag="h_grouped")
             nc.vector.tensor_tensor(
                 out=h_grouped[:].rearrange("p (c i) t -> p c t i", i=2),
                 in0=hidden[(i, g)][:].rearrange("p t (c i) -> p c t i", i=2),
@@ -400,6 +425,22 @@ def tile_atomic_energy_ensemble_d4_kernel(
             )
             hq[(i, g)] = (h_codes, h_planes)
 
+        def scale_rows(i, g):
+            h_plain = work.tile([P, 4, 2 * P], BF16)
+            for t in range(4):
+                nc.scalar.activation(
+                    out=h_plain[:, t, :], in_=hidden[(i, g)][:, t, :], func=ACT.Copy, scale=gain_f32[:, g, t : t + 1]
+                )
+            plain[(i, g)] = h_plain
+
+        def interleave(i, g):
+            h_grouped = work.tile([P, 2 * P, 4], BF16, align_bytes=64, tag="h_grouped")
+            nc.vector.tensor_copy(
+                out=h_grouped[:].rearrange("p (c i) t -> p c t i", i=4),
+                in_=plain[(i, g)][:].rearrange("p t (c i) -> p c t i", i=4),
+            )
+            gained[(i, g)] = h_grouped
+
         def times_gain_half(i, r):
             g = 1
             if r == 0:
@@ -408,7 +449,7 @@ def tile_atomic_energy_ensemble_d4_kernel(
             cols = slice(r * P, (r + 1) * P)
             nc.vector.tensor_tensor(
                 out=gained[(i, g)][:, cols, :].rearrange("p (c i) t -> p c t i", i=2),
-                in0=hidden[(i, g)][:, :, cols].rearrange("p t (c i) -> p c t i", i=2),
+                in0=hidden[(i, g, r)][:].rearrange("p t (c i) -> p c t i", i=2),
                 in1=gain_sb[:, g, :].unsqueeze(1).unsqueeze(3).to_broadcast([P, P // 2, 4, 2]),
                 op=ALU.mult,
             )
@@ -427,7 +468,10 @@ def tile_atomic_energy_ensemble_d4_kernel(
             )
 
         def product_2(i, r):
-            o = o_psum.tile([P, R], F32)
+            if i < UNITS - 1:
+                o = o_psum.tile([P, R], F32)
+            else:
+                o = turn_psum.tile([P, R], F32, tag="turn")
             for g in range(GROUPS):
                 codes, planes = hq[(i, g)]
                 nc.tensor.matmul_mx(
@@ -447,6 +491,7 @@ def tile_atomic_energy_ensemble_d4_kernel(
             nc.sync.dma_start(out=out_view[2 * i + r], in_=energies[:])
 
         wide, groups, xq, zs, hidden, gained, hq, outs = {}, {}, {}, {}, {}, {}, {}, {}
+        plain = {}
         sorted_words = set()
         pending = {"v": [], "s": []}
         for i in range(UNITS):
@@ -522,6 +567,16 @@ def tile_atomic_energy_ensemble_d4_kernel(
             elif name == "D":
                 for n in range(args[0]):
                     heat()
+            elif name == "GF":
+                nc.vector.tensor_copy(out=gain_f32[:], in_=gain_sb[:])
+            elif name == "GS":
+                scale_rows(args[0], args[1])
+            elif name == "GI":
+                interleave(args[0], args[1])
+            elif name == "ZH":
+                product_1_half(args[0], args[1], args[2])
+            elif name == "THH":
+                tanh_half(args[0], args[1], args[2])
             elif name == "GT":
                 times_gain_half(args[0], args[1])
             elif name == "HT":

from contextlib import ExitStack

import concourse.mybir as mybir
from concourse.masks import make_identity

A, K, H, R, B = 2048, 1536, 1024, 512, 128
FLOPS = 2 * A * K * H + 2 * A * H * R

F32 = mybir.dt.float32
BF16 = mybir.dt.bfloat16
I32 = mybir.dt.int32
U32 = mybir.dt.uint32
U8 = mybir.dt.uint8
FP8 = mybir.dt.float8_e4m3fn
FP8X4 = mybir.dt.float8_e4m3fn_x4
FP4X4 = mybir.dt.float4_e2m1fn_x4
ACT = mybir.ActivationFunctionType
ALU = mybir.AluOpType

P = 128
PASSES = K // 512
GROUPS = H // 512
ROWS = A // P
UNITS = ROWS // 2
BLOCKS = K // B

PLAN = {
    "v_rows": [[(0, 0), (0, 1), (0, 2), (1, 0), (1, 1), (1, 2)], [(0, 0), (0, 1), (0, 2), (1, 0)], [(0, 0), (0, 1), (0, 2), (1, 0), (1, 1)], [(0, 0), (0, 1), (0, 2), (1, 0)], [(0, 0), (0, 1), (0, 2), (1, 0)], [(0, 0), (0, 1), (0, 2)], [(0, 0)], [(0, 0), (0, 1), (0, 2), (1, 0), (1, 1)]],
    "psum": (3, 3, 2),
    "steps": [
        ('D', 4),
        ('V', 24),
        ('S', 0),
        ('D', 2),
        ('T1', 'w', 0, 0, 's'),
        ('T1', 'w', 0, 1, 's'),
        ('T1', 'w', 0, 2, 's'),
        ('V', 5),
        ('T1', 'x', 0, 0, 's'),
        ('T1', 'x', 0, 1, 's'),
        ('T1', 'x', 0, 2, 's'),
        ('QW', 0),
        ('S', 4),
        ('D', 1),
        ('T1', 'w', 1, 0, 's'),
        ('T1', 'w', 1, 1, 's'),
        ('T1', 'w', 1, 2, 's'),
        ('QX', 0),
        ('V', 15),
        ('S', 3),
        ('Z', 0, 0),
        ('QW', 1),
        ('V', 7),
        ('S', 5),
        ('T1', 'w', 2, 0, 's'),
        ('T1', 'w', 2, 1, 's'),
        ('T1', 'w', 2, 2, 's'),
        ('TH', 0, 0),
        ('V', 7),
        ('Z', 0, 1),
        ('QW', 2),
        ('T1', 'w', 3, 0, 's'),
        ('T1', 'w', 3, 1, 's'),
        ('T1', 'w', 3, 2, 's'),
        ('TH', 0, 1),
        ('V', 15),
        ('S', 1),
        ('Z', 0, 2),
        ('QW', 3),
        ('V', 3),
        ('T1', 'x', 1, 0, 's'),
        ('T1', 'x', 1, 1, 's'),
        ('T1', 'x', 1, 2, 's'),
        ('TH', 0, 2),
        ('G', 0, 0),
        ('Z', 0, 3),
        ('QX', 1),
        ('V', 8),
        ('H', 0, 0),
        ('TH', 0, 3),
        ('T1', 'x', 2, 0, 's'),
        ('T1', 'x', 2, 1, 's'),
        ('T1', 'x', 2, 2, 's'),
        ('Q1', 2, 0),
        ('Z', 1, 0),
        ('TH', 1, 0),
        ('G', 0, 1),
        ('Q1', 2, 1),
        ('Q1', 2, 2),
        ('Z', 1, 1),
        ('TH', 1, 1),
        ('S', 2),
        ('H', 0, 1),
        ('G', 1, 0),
        ('Z', 1, 2),
        ('TH', 1, 2),
        ('V', 6),
        ('S', 10),
        ('H', 1, 0),
        ('Z', 1, 3),
        ('TH', 1, 3),
        ('V', 4),
        ('O', 0, 0),
        ('O', 0, 1),
        ('A', 0, 0),
        ('G', 1, 1),
        ('A', 0, 1),
        ('H', 1, 1),
        ('TX', 3, 'sss'),
        ('Q1', 3, 0),
        ('Z', 2, 0),
        ('TH', 2, 0),
        ('Q1', 3, 1),
        ('Q1', 3, 2),
        ('Z', 2, 1),
        ('TH', 2, 1),
        ('S', 2),
        ('G', 2, 0),
        ('Z', 2, 2),
        ('TH', 2, 2),
        ('V', 6),
        ('S', 10),
        ('H', 2, 0),
        ('Z', 2, 3),
        ('TH', 2, 3),
        ('V', 4),
        ('O', 1, 0),
        ('O', 1, 1),
        ('A', 1, 0),
        ('G', 2, 1),
        ('A', 1, 1),
        ('H', 2, 1),
        ('TX', 4, 'sss'),
        ('Q1', 4, 0),
        ('Z', 3, 0),
        ('TH', 3, 0),
        ('Q1', 4, 1),
        ('Q1', 4, 2),
        ('Z', 3, 1),
        ('TH', 3, 1),
        ('S', 2),
        ('G', 3, 0),
        ('Z', 3, 2),
        ('TH', 3, 2),
        ('V', 6),
        ('S', 10),
        ('H', 3, 0),
        ('Z', 3, 3),
        ('TH', 3, 3),
        ('V', 4),
        ('O', 2, 0),
        ('O', 2, 1),
        ('A', 2, 0),
        ('G', 3, 1),
        ('A', 2, 1),
        ('H', 3, 1),
        ('TX', 5, 'sss'),
        ('Q1', 5, 0),
        ('Z', 4, 0),
        ('TH', 4, 0),
        ('Q1', 5, 1),
        ('Q1', 5, 2),
        ('Z', 4, 1),
        ('TH', 4, 1),
        ('S', 2),
        ('G', 4, 0),
        ('Z', 4, 2),
        ('TH', 4, 2),
        ('V', 6),
        ('S', 10),
        ('H', 4, 0),
        ('Z', 4, 3),
        ('TH', 4, 3),
        ('V', 4),
        ('O', 3, 0),
        ('O', 3, 1),
        ('A', 3, 0),
        ('G', 4, 1),
        ('A', 3, 1),
        ('H', 4, 1),
        ('TX', 6, 'sss'),
        ('Q1', 6, 0),
        ('Z', 5, 0),
        ('TH', 5, 0),
        ('Q1', 6, 1),
        ('Q1', 6, 2),
        ('Z', 5, 1),
        ('TH', 5, 1),
        ('S', 2),
        ('G', 5, 0),
        ('Z', 5, 2),
        ('TH', 5, 2),
        ('V', 6),
        ('S', 10),
        ('H', 5, 0),
        ('Z', 5, 3),
        ('TH', 5, 3),
        ('V', 4),
        ('O', 4, 0),
        ('O', 4, 1),
        ('A', 4, 0),
        ('G', 5, 1),
        ('A', 4, 1),
        ('H', 5, 1),
        ('TX', 7, 'sss'),
        ('Q1', 7, 0),
        ('Z', 6, 0),
        ('TH', 6, 0),
        ('Q1', 7, 1),
        ('Q1', 7, 2),
        ('Z', 6, 1),
        ('TH', 6, 1),
        ('G', 6, 0),
        ('Z', 6, 2),
        ('TH', 6, 2),
        ('H', 6, 0),
        ('Z', 6, 3),
        ('TH', 6, 3),
        ('O', 5, 0),
        ('O', 5, 1),
        ('A', 5, 0),
        ('G', 6, 1),
        ('A', 5, 1),
        ('H', 6, 1),
        ('Z', 7, 0),
        ('TH', 7, 0),
        ('Z', 7, 1),
        ('TH', 7, 1),
        ('ZH', 7, 0, 0),
        ('THH', 7, 0, 0),
        ('G', 7, 0),
        ('ZH', 7, 0, 1),
        ('THH', 7, 0, 1),
        ('H', 7, 0),
        ('ZH', 7, 1, 0),
        ('THH', 7, 1, 0),
        ('GT', 7, 0),
        ('ZH', 7, 1, 1),
        ('THH', 7, 1, 1),
        ('O', 6, 0),
        ('O', 6, 1),
        ('HT', 7, 0),
        ('GT', 7, 1),
        ('A', 6, 0),
        ('HT', 7, 1),
        ('A', 6, 1),
        ('O', 7, 0),
        ('O', 7, 1),
        ('A', 7, 0),
        ('A', 7, 1),
    ],
}


def tile_atomic_energy_ensemble_d4_kernel(
    tc, x_bytes, x_scale, w, bias, gain, v_words, v_scales, offset, out
):
    nc = tc.nc
    with ExitStack() as ctx:
        keep = ctx.enter_context(tc.tile_pool(name="keep", bufs=1))
        work = ctx.enter_context(tc.tile_pool(name="work", bufs=3))
        turn_psum = ctx.enter_context(tc.psum_pool(name="turn_psum", bufs=PLAN["psum"][0]))
        z_psum = ctx.enter_context(tc.psum_pool(name="z_psum", bufs=PLAN["psum"][1]))
        o_psum = ctx.enter_context(tc.psum_pool(name="o_psum", bufs=PLAN["psum"][2]))

        ident = keep.tile([P, P], F32)
        scale = keep.tile([P, ROWS, BLOCKS], F32)
        x_raw = keep.tile([P, ROWS, K], U8)
        w_raw = keep.tile([P, 4, 2, K], BF16, align_bytes=64)
        w_codes = keep.tile([P, 4, PASSES, 2 * P], U32, align_bytes=64)
        w_planes = keep.tile([P, 4, PASSES, 2 * P], U8, align_bytes=64)
        bias_sb = keep.tile([P, GROUPS, 4], BF16)
        gain_sb = keep.tile([P, GROUPS, 4], BF16)
        gain_f32 = keep.tile([P, GROUPS, 4], F32)
        v_sb = keep.tile([P, GROUPS, 2 * R], U8, align_bytes=64)
        v_planes = keep.tile([P, GROUPS, R], U8, align_bytes=64)
        offset_sb = keep.tile([P, R], BF16)
        warm = keep.tile([P, 1], F32)
        zeros = keep.tile([P, 5 * P], BF16)

        x_view = x_bytes.rearrange("(p n) k -> p n k", n=ROWS)
        w_view = w.rearrange("(g m t) k -> g t m k", m=P, t=4)
        out_view = out.rearrange("(p n) r -> n p r", n=ROWS)

        def load_x(i):
            nc.sync.dma_start(out=x_raw[:, 2 * i : 2 * i + 2, :], in_=x_view[:, 2 * i : 2 * i + 2, :])

        def load_w(j, r):
            g, h = divmod(j, 2)
            nc.sync.dma_start(out=w_raw[:, j, r, :], in_=w_view[g, 2 * h + r])

        def widen(i, r, b, engine):
            n = 2 * i + r
            src = x_raw[:, n, B * b : B * (b + 1)].bitcast(FP8)
            s = scale[:, n, b : b + 1]
            if engine == "v":
                c, q = divmod(b, 4)
                pairs = wide[i][:, r, 512 * c : 512 * (c + 1)].rearrange("p (u a e) -> p a u e", u=2, e=2)
                nc.vector.tensor_scalar(
                    out=pairs[:, 32 * q : 32 * (q + 1), :, :],
                    in0=src.rearrange("p (a u e) -> p a u e", u=2, e=2),
                    scalar1=s,
                    scalar2=None,
                    op0=ALU.mult,
                )
                sorted_words.add((i, r, c))
            else:
                nc.scalar.activation(out=wide[i][:, r, B * b : B * (b + 1)], in_=src, func=ACT.Copy, scale=s)

        def new_wide(i):
            x_wide = work.tile([P, 2, K], BF16, align_bytes=64)
            wide[i] = x_wide

        def turn(src, key, c, engine):
            bank = turn_psum.tile([P, 2, 2, P], F32, tag="turn")
            for r in range(2):
                words = src[:, r, :].bitcast(F32)
                for u in range(2):
                    if key[0] == "x" and (key[1], r, c) in sorted_words:
                        picked = words[:, 256 * c + P * u : 256 * c + P * (u + 1)]
                    else:
                        picked = words[:, 256 * c + u : 256 * (c + 1) : 2]
                    nc.tensor.transpose(bank[:, r, u, :], picked, ident[:])
            grouped = work.tile([P, 2, P, 4], BF16, align_bytes=64, bufs=9)
            o = grouped[:].bitcast(F32)
            i_ = bank[:].rearrange("p r u n -> p r n u")
            if engine == "v":
                nc.vector.tensor_copy(out=o, in_=i_)
            else:
                nc.scalar.copy(out=o, in_=i_)
            groups[(key, c)] = grouped

        def quantize(key, c, codes, planes):
            nc.vector.quantize_mx(
                out=codes.bitcast(FP8X4),
                scales=planes,
                in_=groups[(key, c)][:].rearrange("p r n t -> p (r n t)"),
            )

        def quantize_x(i, c):
            if i not in xq:
                x_codes = work.tile([P, PASSES, 2 * P], U32, align_bytes=64)
                x_planes = work.tile([P, PASSES, 2 * P], U8, align_bytes=64)
                xq[i] = (x_codes, x_planes)
            quantize(("x", i), c, xq[i][0][:, c, :], xq[i][1][:, c, :])

        def quantize_w(j, c):
            quantize(("w", j), c, w_codes[:, j, c, :], w_planes[:, j, c, :])

        def product_1(i, j):
            z = z_psum.tile([P, 2, 2 * P], F32, tag="z")
            for r in range(2):
                for c in range(PASSES):
                    nc.tensor.matmul_mx(
                        out=z[:, r, :],
                        lhsT=w_codes[:, j, c, r * P : (r + 1) * P].bitcast(FP8X4),
                        lhsT_scale=w_planes[:, j, c, r * P : (r + 1) * P],
                        rhs=xq[i][0][:, c, :].bitcast(FP8X4),
                        rhs_scale=xq[i][1][:, c, :],
                        start=(c == 0),
                        stop=(c == PASSES - 1),
                    )
            zs[(i, j)] = z

        def tanh(i, j):
            g, h = divmod(j, 2)
            if (i, g) not in hidden:
                h_tanh = work.tile([P, 4, 2 * P], F32)
                hidden[(i, g)] = h_tanh
            for r in range(2):
                t = 2 * h + r
                nc.scalar.activation(
                    out=hidden[(i, g)][:, t, :], in_=zs[(i, j)][:, r, :], func=ACT.Tanh, bias=bias_sb[:, g, t : t + 1]
                )

        def product_1_half(i, r, h):
            if r == 0:
                z_half = z_psum.tile([P, 2, P], F32, tag="z")
            else:
                z_half = turn_psum.tile([P, 2, P], F32, tag="turn")
            cols = slice(r * P, (r + 1) * P)
            for s in range(2):
                for c in range(PASSES):
                    nc.tensor.matmul_mx(
                        out=z_half[:, s, :],
                        lhsT=w_codes[:, 2 + h, c, s * P : (s + 1) * P].bitcast(FP8X4),
                        lhsT_scale=w_planes[:, 2 + h, c, s * P : (s + 1) * P],
                        rhs=xq[i][0][:, c, cols].bitcast(FP8X4),
                        rhs_scale=xq[i][1][:, c, cols],
                        start=(c == 0),
                        stop=(c == PASSES - 1),
                    )
            zs[(i, r, h)] = z_half

        def tanh_half(i, r, h):
            if (i, 1, r) not in hidden:
                h_tanh_half = work.tile([P, 4, P], F32, bufs=2)
                hidden[(i, 1, r)] = h_tanh_half
            for s in range(2):
                t = 2 * h + s
                nc.scalar.activation(
                    out=hidden[(i, 1, r)][:, t, :],
                    in_=zs[(i, r, h)][:, s, :],
                    func=ACT.Tanh,
                    bias=bias_sb[:, 1, t : t + 1],
                )

        def times_gain(i, g):
            h_grouped = work.tile([P, 2 * P, 4], BF16, align_bytes=64, tag="h_grouped")
            nc.vector.tensor_tensor(
                out=h_grouped[:].rearrange("p (c i) t -> p c t i", i=2),
                in0=hidden[(i, g)][:].rearrange("p t (c i) -> p c t i", i=2),
                in1=gain_sb[:, g, :].unsqueeze(1).unsqueeze(3).to_broadcast([P, P, 4, 2]),
                op=ALU.mult,
            )
            gained[(i, g)] = h_grouped

        def quantize_h(i, g):
            h_codes = work.tile([P, 2 * P], U32, align_bytes=64, bufs=6)
            h_planes = work.tile([P, 2 * P], U8, align_bytes=64, bufs=6)
            nc.vector.quantize_mx(
                out=h_codes[:].bitcast(FP8X4),
                scales=h_planes[:],
                in_=gained[(i, g)][:].rearrange("p n t -> p (n t)"),
            )
            hq[(i, g)] = (h_codes, h_planes)

        def scale_rows(i, g):
            h_plain = work.tile([P, 4, 2 * P], BF16)
            for t in range(4):
                nc.scalar.activation(
                    out=h_plain[:, t, :], in_=hidden[(i, g)][:, t, :], func=ACT.Copy, scale=gain_f32[:, g, t : t + 1]
                )
            plain[(i, g)] = h_plain

        def interleave(i, g):
            h_grouped = work.tile([P, 2 * P, 4], BF16, align_bytes=64, tag="h_grouped")
            nc.vector.tensor_copy(
                out=h_grouped[:].rearrange("p (c i) t -> p c t i", i=4),
                in_=plain[(i, g)][:].rearrange("p t (c i) -> p c t i", i=4),
            )
            gained[(i, g)] = h_grouped

        def times_gain_half(i, r):
            g = 1
            if r == 0:
                h_grouped_t = work.tile([P, 2 * P, 4], BF16, align_bytes=64, bufs=1)
                gained[(i, g)] = h_grouped_t
            cols = slice(r * P, (r + 1) * P)
            nc.vector.tensor_tensor(
                out=gained[(i, g)][:, cols, :].rearrange("p (c i) t -> p c t i", i=2),
                in0=hidden[(i, g, r)][:].rearrange("p t (c i) -> p c t i", i=2),
                in1=gain_sb[:, g, :].unsqueeze(1).unsqueeze(3).to_broadcast([P, P // 2, 4, 2]),
                op=ALU.mult,
            )

        def quantize_h_half(i, r):
            g = 1
            if r == 0:
                h_codes_t = work.tile([P, 2 * P], U32, align_bytes=64, bufs=1)
                h_planes_t = work.tile([P, 2 * P], U8, align_bytes=64, bufs=1)
                hq[(i, g)] = (h_codes_t, h_planes_t)
            cols = slice(r * P, (r + 1) * P)
            nc.vector.quantize_mx(
                out=hq[(i, g)][0][:, cols].bitcast(FP8X4),
                scales=hq[(i, g)][1][:, cols],
                in_=gained[(i, g)][:, cols, :].rearrange("p n t -> p (n t)"),
            )

        def product_2(i, r):
            if i < UNITS - 1:
                o = o_psum.tile([P, R], F32)
            else:
                o = turn_psum.tile([P, R], F32, tag="turn")
            for g in range(GROUPS):
                codes, planes = hq[(i, g)]
                nc.tensor.matmul_mx(
                    out=o[:],
                    lhsT=codes[:, r * P : (r + 1) * P].bitcast(FP8X4),
                    lhsT_scale=planes[:, r * P : (r + 1) * P],
                    rhs=v_sb[:, g, :].bitcast(FP4X4),
                    rhs_scale=v_planes[:, g, :],
                    start=(g == 0),
                    stop=(g == GROUPS - 1),
                )
            outs[(i, r)] = o

        def finish(i, r):
            energies = work.tile([P, R], F32, bufs=4)
            nc.vector.tensor_tensor(out=energies[:], in0=outs[(i, r)][:], in1=offset_sb[:], op=ALU.add)
            nc.sync.dma_start(out=out_view[2 * i + r], in_=energies[:])

        wide, groups, xq, zs, hidden, gained, hq, outs = {}, {}, {}, {}, {}, {}, {}, {}
        plain = {}
        sorted_words = set()
        pending = {"v": [], "s": []}
        for i in range(UNITS):
            for c in range(PASSES):
                for r in range(2):
                    for q in range(4):
                        pending["v" if (r, c) in PLAN["v_rows"][i] else "s"].append((i, r, 4 * c + q))

        def fill(engine, count):
            for n in range(min(count, len(pending[engine]))):
                i, r, b = pending[engine].pop(0)
                if i not in wide:
                    new_wide(i)
                widen(i, r, b, engine)

        def flush(i, c):
            for engine in ("v", "s"):
                while pending[engine] and (pending[engine][0][0] < i or (pending[engine][0][0] == i and pending[engine][0][2] < 4 * (c + 1))):
                    fill(engine, 1)

        def turn_x(i, engines):
            for c in range(PASSES):
                flush(i, c)
                turn(wide[i], ("x", i), c, engines[c])

        def turn_w(j, engines):
            for c in range(PASSES):
                turn(w_raw[:, j, :, :], ("w", j), c, engines[c])

        def heat():
            bank = z_psum.tile([P, 512], F32, tag="z")
            nc.tensor.matmul(bank[:], lhsT=zeros[:, :P], rhs=zeros[:, P:], start=True, stop=True)

        def run(step):
            name, args = step[0], step[1:]
            if name == "V":
                fill("v", args[0])
            elif name == "S":
                fill("s", args[0])
            elif name == "TW":
                turn_w(args[0], args[1])
            elif name == "TX":
                turn_x(args[0], args[1])
            elif name == "T1":
                kind, unit, c, engine = args
                if kind == "w":
                    turn(w_raw[:, unit, :, :], ("w", unit), c, engine)
                else:
                    flush(unit, c)
                    turn(wide[unit], ("x", unit), c, engine)
            elif name == "QW1":
                quantize_w(args[0], args[1])
            elif name == "QW":
                for c in range(PASSES):
                    quantize_w(args[0], c)
            elif name == "QX":
                for c in range(PASSES):
                    quantize_x(args[0], c)
            elif name == "Q1":
                quantize_x(args[0], args[1])
            elif name == "Z":
                product_1(args[0], args[1])
            elif name == "TH":
                tanh(args[0], args[1])
            elif name == "G":
                times_gain(args[0], args[1])
            elif name == "H":
                quantize_h(args[0], args[1])
            elif name == "O":
                product_2(args[0], args[1])
            elif name == "A":
                finish(args[0], args[1])
            elif name == "D":
                for n in range(args[0]):
                    heat()
            elif name == "GF":
                nc.vector.tensor_copy(out=gain_f32[:], in_=gain_sb[:])
            elif name == "GS":
                scale_rows(args[0], args[1])
            elif name == "GI":
                interleave(args[0], args[1])
            elif name == "ZH":
                product_1_half(args[0], args[1], args[2])
            elif name == "THH":
                tanh_half(args[0], args[1], args[2])
            elif name == "GT":
                times_gain_half(args[0], args[1])
            elif name == "HT":
                quantize_h_half(args[0], args[1])

        with tc.manual_schedule():
            nc.vector.memset(zeros[:], 0.0)
            nc.vector.memset(warm[:], 0.0)
            nc.scalar.activation(out=warm[:], in_=warm[:], func=ACT.Tanh)
            make_identity(nc, ident[:])
            nc.gpsimd.memset(v_planes[:].rearrange("p g n -> p (g n)").bitcast(I32), 0)

            nc.sync.dma_start(out=scale[:], in_=x_scale.rearrange("(p n) j -> p n j", n=ROWS))
            load_x(0)
            load_w(0, 0)
            load_w(0, 1)
            load_w(1, 0)
            load_w(1, 1)
            nc.sync.dma_start(out=bias_sb[:], in_=bias.rearrange("(g p t) -> p g t", p=P, t=4))
            load_x(1)
            load_w(2, 0)
            load_w(2, 1)
            load_x(2)
            nc.sync.dma_start(out=gain_sb[:], in_=gain.rearrange("(g p t) -> p g t", p=P, t=4))
            load_w(3, 0)
            load_w(3, 1)
            for q in range(4):
                nc.sync.dma_start(
                    out=v_planes[32 * q : 32 * q + 4, :, :].bitcast(I32),
                    in_=v_scales[:, 4 * q : 4 * q + 4, :].rearrange("g q n -> q g n").bitcast(I32),
                )
            nc.sync.dma_start(out=v_sb[:].bitcast(I32), in_=v_words.rearrange("g p n -> p g n").bitcast(I32))
            load_x(3)
            nc.sync.dma_start(out=offset_sb[:], in_=offset.partition_broadcast(P))
            for i in range(4, UNITS):
                load_x(i)

            for step in PLAN["steps"]:
                run(step)
